import numpy as np
import ml_dtypes


def mxq(x, axis, fmt="e4m3"):
    dtype, down = {"e4m3": (ml_dtypes.float8_e4m3fn, 7), "e5m2": (ml_dtypes.float8_e5m2, 14)}[fmt]
    v = np.moveaxis(np.asarray(x, np.float32).astype(ml_dtypes.bfloat16).astype(np.float64), axis, -1)
    blocks = v.reshape(v.shape[:-1] + (-1, 32))
    amax = np.abs(blocks).max(-1, keepdims=True)
    byte = np.maximum(np.where(amax > 0, np.frexp(amax)[1] - 1 + 127, 0) - down, 1)
    scale = np.exp2(byte - 127.0)
    codes = (blocks / scale).astype(np.float32).astype(dtype).astype(np.float64)
    return np.moveaxis((codes * scale).reshape(v.shape), -1, axis)


WIDE = False


def mx_kscale(k):
    if not WIDE:
        return np.ones(k)
    levels = np.array([10, -10, 5, -5, 0])
    if k % 512:
        return np.exp2(np.random.permutation(np.resize(levels, k // 32))).repeat(32)
    a = np.empty((k // 512, 16))
    for p in range(k // 512):
        a[p, :8] = np.random.permutation(np.resize(levels, 8))
        for g in range(8):
            far = levels[np.abs(levels - a[p, g]) >= 10]
            a[p, g + 8] = far[np.random.randint(len(far))]
    return np.exp2(a.ravel()).repeat(32)


def f64(x):
    return np.asarray(x).astype(np.float64)


def striped(idx):
    return np.tile(np.asarray(idx).reshape(-1, 16).T, (8, 1)).astype(np.uint16)


def unstriped(offs):
    return offs[:16].T.reshape(-1).astype(np.int64)


B, N, T, D, DV, NQ = 2, 256, 2048, 1024, 0, 256


def setup_inputs():
    n = np.random.standard_normal
    idx = np.sort(np.random.permutation(T)[:B * N].reshape(B, N), axis=1).reshape(-1)
    s = mx_kscale(D)[:, None]
    r = np.random.uniform(0.5, 2.0, T)
    return {
        "qT": (n((B, D, NQ)) * s * (1.00 / np.sqrt(D))).astype(np.float32),
        "kT": (n((D, T)) / s / r).astype(np.float32),
        "ts": np.tile(r, (128, 1)).astype(np.float32),
        "offs": striped(idx),
    }


def reference(qT, kT, ts, offs):
    idx = unstriped(offs)
    pick = lambda x: x[:, idx].reshape(x.shape[0], B, N).transpose(1, 0, 2)
    a = mxq(f64(qT), 1, "e4m3").transpose(0, 2, 1) @ mxq(pick(f64(kT)), 1, "e4m3")
    a = a * pick(f64(ts))[:, :1, :]
    out = np.zeros((B, NQ, T))
    for b in range(B):
        out[b][:, idx[b * N:(b + 1) * N]] = a[b]
    return out

@@ -1,0 +1,156 @@
+from contextlib import ExitStack
+
+import concourse.mybir as mybir
+from concourse.masks import make_identity
+
+B, D, NQ, T, N = 2, 1024, 256, 2048, 256
+P = 128
+PACK = 4
+PASSES = D // (P * PACK)
+QT = NQ // P
+COLS = N // 16
+
+F32 = mybir.dt.float32
+BF16 = mybir.dt.bfloat16
+U32 = mybir.dt.uint32
+U16 = mybir.dt.uint16
+U8 = mybir.dt.uint8
+FP8X4 = mybir.dt.float8_e4m3fn_x4
+MULT = mybir.AluOpType.mult
+
+FLOPS = 2 * B * NQ * N * D
+BYTES = 4 * (B * D * NQ + D * T + T + B * NQ * T) + 2 * P * B * COLS
+
+
+def tile_attend_sddmm_srt_ts_kernel(tc, qT, kT, ts, offs, out):
+    nc = tc.nc
+    with ExitStack() as ctx:
+        keep = ctx.enter_context(tc.tile_pool(name="keep", bufs=1))
+        psum = ctx.enter_context(tc.psum_pool(name="psum", bufs=1))
+
+        offsets = keep.tile([P, B * COLS], U16, name="offsets")
+        nc.sync.dma_start(offsets[:], offs)
+        ts_cols = keep.tile([P, T // P], F32, name="ts_cols")
+        nc.sync.dma_start(ts_cols[:], ts[0, :].rearrange("(p i) -> p i", i=T // P))
+
+        q_rows = qT.rearrange("b (g p j) w -> b g p j w", p=P, j=PACK)
+        k_rows = kT.rearrange("(g p j) w -> g j p w", p=P, j=PACK)
+
+        q_raw = {}
+        k_raw = {}
+
+        def load_q(b, g):
+            t = keep.tile([P, PACK, NQ], F32, name=f"q_raw{b}{g}")
+            nc.sync.dma_start(t[:], q_rows[b, g])
+            q_raw[b, g] = t
+
+        def load_k(g, j):
+            t = keep.tile([P, T], F32, name=f"k_raw{g}{j}")
+            nc.sync.dma_start(t[:], k_rows[g, j])
+            k_raw[g, j] = t
+
+        load_q(0, 0)
+        for g in range(PASSES):
+            for j in range(PACK):
+                load_k(g, j)
+        load_q(0, 1)
+        load_q(1, 0)
+        load_q(1, 1)
+
+        ident = keep.tile([P, P], F32, name="ident")
+        make_identity(nc, ident[:])
+
+        windows = {}
+        for b in range(B):
+            for m in range(QT):
+                w = keep.tile([P, T], F32, name=f"window{b}{m}")
+                nc.vector.memset(w[:], 0.0)
+                windows[b, m] = w
+
+        ts_all = keep.tile([P, T], F32, name="ts_all")
+        ts_view = ts_all[:].rearrange("p (n i) -> p n i", i=T // P)
+        for h in range(4):
+            bank = psum.tile([P, 4, P], F32, name=f"ts_bank{h}")
+            for i in range(4):
+                c = 4 * h + i
+                nc.tensor.transpose(bank[:, i, :], ts_cols[:, c : c + 1].to_broadcast([P, P]), ident[:])
+            nc.scalar.copy(out=ts_view[:, :, 4 * h : 4 * h + 4], in_=bank[:].rearrange("p i n -> p n i"))
+        ts_got = keep.tile([P, B * N], F32, name="ts_got")
+        nc.vector.tensor_copy(ts_got[:], ts_all[:].indirect(offsets[:]))
+
+        q_codes, q_scales = {}, {}
+
+        def cast_q(b, g):
+            t = keep.tile([P, NQ, PACK], BF16, name=f"q_grouped{b}{g}", align_bytes=64)
+            nc.scalar.copy(out=t[:], in_=q_raw[b, g][:].rearrange("p j w -> p w j"))
+            return t
+
+        def quant(grouped, width, name):
+            codes = keep.tile([P, width], U32, name=f"{name}_codes", align_bytes=64)
+            scales = keep.tile([P, width], U8, name=f"{name}_scales", align_bytes=64)
+            nc.vector.quantize_mx(
+                out=codes[:].bitcast(FP8X4), scales=scales[:], in_=grouped[:].rearrange("p w j -> p (w j)")
+            )
+            return codes, scales
+
+        def mm(acc, q, m, k, k0, g):
+            nc.tensor.matmul_mx(
+                out=acc[:],
+                lhsT=q[0][:, m * P : (m + 1) * P].bitcast(FP8X4),
+                lhsT_scale=q[1][:, m * P : (m + 1) * P],
+                rhs=k[0][:, k0 : k0 + N].bitcast(FP8X4),
+                rhs_scale=k[1][:, k0 : k0 + N],
+                start=(g == 0),
+                stop=(g == PASSES - 1),
+            )
+
+        acc = {}
+        for b in range(B):
+            for m in range(QT):
+                a = psum.tile([P, N], F32, name=f"acc{b}{m}")
+                acc[b, m] = a
+
+        q00 = quant(cast_q(0, 0), NQ, "q00")
+        grouped0 = keep.tile([P, B * N, PACK], BF16, name="grouped0", align_bytes=64)
+        for j in range(PACK):
+            nc.vector.tensor_copy(grouped0[:, :, j], k_raw[0, j][:].indirect(offsets[:]))
+        k0 = quant(grouped0, B * N, "k0")
+        for m in range(QT):
+            mm(acc[0, m], q00, m, k0, 0, 0)
+
+        grouped1 = []
+        for b in range(B):
+            t = keep.tile([P, N, PACK], BF16, name=f"grouped1{b}", align_bytes=64)
+            grouped1.append(t)
+        for j in range(PACK):
+            for b in range(B):
+                nc.vector.tensor_copy(
+                    grouped1[b][:, :, j], k_raw[1, j][:].indirect(offsets[:, b * COLS : (b + 1) * COLS])
+                )
+                if j == PACK - 1 and b == 0:
+                    k10 = quant(grouped1[0], N, "k10")
+                    q01 = quant(cast_q(0, 1), NQ, "q01")
+        k11 = quant(grouped1[1], N, "k11")
+
+        def finish(b, m):
+            s = keep.tile([P, N], F32, name=f"scores{b}{m}")
+            nc.scalar.copy(out=s[:], in_=acc[b, m][:])
+            nc.vector.tensor_tensor(
+                windows[b, m][:].indirect(offsets[:, b * COLS : (b + 1) * COLS]),
+                s[:],
+                ts_got[:, b * N : (b + 1) * N],
+                MULT,
+            )
+            nc.sync.dma_start(out[b, m * P : (m + 1) * P, :], windows[b, m][:])
+
+        for m in range(QT):
+            mm(acc[0, m], q01, m, k10, 0, 1)
+            finish(0, m)
+
+        q10 = quant(cast_q(1, 0), NQ, "q10")
+        for m in range(QT):
+            mm(acc[1, m], q10, m, k0, N, 0)
+        q11 = quant(cast_q(1, 1), NQ, "q11")
+        for m in range(QT):
+            mm(acc[1, m], q11, m, k11, 0, 1)
+            finish(1, m)

@@ -39,23 +39,24 @@ def tile_attend_sddmm_srt_ts_kernel(tc, qT, kT, ts, offs, out):
         q_raw = {}
         k_raw = {}
 
-        def load_q(b, g):
-            t = keep.tile([P, PACK, NQ], F32, name=f"q_raw{b}{g}")
-            nc.sync.dma_start(t[:], q_rows[b, g])
-            q_raw[b, g] = t
+        def load_q(b, m, g):
+            t = keep.tile([P, PACK, P], F32, name=f"q_raw{b}{m}{g}")
+            nc.sync.dma_start(t[:], q_rows[b, g, :, :, m * P : (m + 1) * P])
+            q_raw[b, m, g] = t
 
         def load_k(g, j):
             t = keep.tile([P, T], F32, name=f"k_raw{g}{j}")
             nc.sync.dma_start(t[:], k_rows[g, j])
             k_raw[g, j] = t
 
-        load_q(0, 0)
+        load_q(0, 0, 0)
         for g in range(PASSES):
             for j in range(PACK):
                 load_k(g, j)
-        load_q(0, 1)
-        load_q(1, 0)
-        load_q(1, 1)
+        load_q(0, 0, 1)
+        for b, m in ((0, 1), (1, 0), (1, 1)):
+            for g in range(PASSES):
+                load_q(b, m, g)
 
         ident = keep.tile([P, P], F32, name="ident")
         make_identity(nc, ident[:])
@@ -64,7 +65,7 @@ def tile_attend_sddmm_srt_ts_kernel(tc, qT, kT, ts, offs, out):
         for b in range(B):
             for m in range(QT):
                 w = keep.tile([P, T], F32, name=f"window{b}{m}")
-                nc.vector.memset(w[:], 0.0)
+                (nc.vector if b == 0 else nc.gpsimd).memset(w[:], 0.0)
                 windows[b, m] = w
 
         ts_all = keep.tile([P, T], F32, name="ts_all")
@@ -78,79 +79,106 @@ def tile_attend_sddmm_srt_ts_kernel(tc, qT, kT, ts, offs, out):
         ts_got = keep.tile([P, B * N], F32, name="ts_got")
         nc.vector.tensor_copy(ts_got[:], ts_all[:].indirect(offsets[:]))
 
-        q_codes, q_scales = {}, {}
-
-        def cast_q(b, g):
-            t = keep.tile([P, NQ, PACK], BF16, name=f"q_grouped{b}{g}", align_bytes=64)
-            nc.scalar.copy(out=t[:], in_=q_raw[b, g][:].rearrange("p j w -> p w j"))
-            return t
-
         def quant(grouped, width, name):
             codes = keep.tile([P, width], U32, name=f"{name}_codes", align_bytes=64)
             scales = keep.tile([P, width], U8, name=f"{name}_scales", align_bytes=64)
-            nc.vector.quantize_mx(
-                out=codes[:].bitcast(FP8X4), scales=scales[:], in_=grouped[:].rearrange("p w j -> p (w j)")
-            )
+            nc.vector.quantize_mx(out=codes[:].bitcast(FP8X4), scales=scales[:], in_=grouped)
             return codes, scales
 
-        def mm(acc, q, m, k, k0, g):
+        def mm(acc, q, q0, k, k0, g):
             nc.tensor.matmul_mx(
                 out=acc[:],
-                lhsT=q[0][:, m * P : (m + 1) * P].bitcast(FP8X4),
-                lhsT_scale=q[1][:, m * P : (m + 1) * P],
+                lhsT=q[0][:, q0 : q0 + P].bitcast(FP8X4),
+                lhsT_scale=q[1][:, q0 : q0 + P],
                 rhs=k[0][:, k0 : k0 + N].bitcast(FP8X4),
                 rhs_scale=k[1][:, k0 : k0 + N],
                 start=(g == 0),
                 stop=(g == PASSES - 1),
             )
 
-        acc = {}
+        def offs_of(b):
+            return offsets[:, b * COLS : (b + 1) * COLS]
+
+        acc, q_grouped = {}, {}
         for b in range(B):
             for m in range(QT):
                 a = psum.tile([P, N], F32, name=f"acc{b}{m}")
                 acc[b, m] = a
+                t = keep.tile([P, PASSES, P, PACK], BF16, name=f"q_grouped{b}{m}", align_bytes=64)
+                q_grouped[b, m] = t
 
-        q00 = quant(cast_q(0, 0), NQ, "q00")
-        grouped0 = keep.tile([P, B * N, PACK], BF16, name="grouped0", align_bytes=64)
+        def cast_q(b, m, g, engine):
+            src = q_raw[b, m, g][:].rearrange("p j w -> p w j")
+            if engine == "scalar":
+                nc.scalar.copy(out=q_grouped[b, m][:, g], in_=src)
+            else:
+                nc.vector.tensor_copy(q_grouped[b, m][:, g], src)
+
+        def q_flat(b, m):
+            return q_grouped[b, m][:].rearrange("p g w j -> p (g w j)")
+
+        cast_q(0, 0, 0, "scalar")
+        q00 = quant(q_flat(0, 0)[:, 0 : P * PACK], P, "q00")
+        k_grouped0 = keep.tile([P, B * N, PACK], BF16, name="k_grouped0", align_bytes=64)
         for j in range(PACK):
-            nc.vector.tensor_copy(grouped0[:, :, j], k_raw[0, j][:].indirect(offsets[:]))
-        k0 = quant(grouped0, B * N, "k0")
-        for m in range(QT):
-            mm(acc[0, m], q00, m, k0, 0, 0)
+            nc.vector.tensor_copy(k_grouped0[:, :, j], k_raw[0, j][:].indirect(offsets[:]))
+        k0 = quant(k_grouped0[:].rearrange("p w j -> p (w j)"), B * N, "k0")
+        mm(acc[0, 0], q00, 0, k0, 0, 0)
 
-        grouped1 = []
+        k_grouped1 = []
         for b in range(B):
-            t = keep.tile([P, N, PACK], BF16, name=f"grouped1{b}", align_bytes=64)
-            grouped1.append(t)
-        for j in range(PACK):
+            t = keep.tile([P, N, PACK], BF16, name=f"k_grouped1{b}", align_bytes=64)
+            k_grouped1.append(t)
+        for j in range(PACK - 1):
             for b in range(B):
-                nc.vector.tensor_copy(
-                    grouped1[b][:, :, j], k_raw[1, j][:].indirect(offsets[:, b * COLS : (b + 1) * COLS])
-                )
-                if j == PACK - 1 and b == 0:
-                    k10 = quant(grouped1[0], N, "k10")
-                    q01 = quant(cast_q(0, 1), NQ, "q01")
-        k11 = quant(grouped1[1], N, "k11")
+                nc.vector.tensor_copy(k_grouped1[b][:, :, j], k_raw[1, j][:].indirect(offs_of(b)))
 
-        def finish(b, m):
-            s = keep.tile([P, N], F32, name=f"scores{b}{m}")
-            nc.scalar.copy(out=s[:], in_=acc[b, m][:])
+        def last_plane(b):
+            j = PACK - 1
+            nc.vector.tensor_copy(k_grouped1[b][:, :, j], k_raw[1, j][:].indirect(offs_of(b)))
+
+        def quant_k1(b):
+            return quant(k_grouped1[b][:].rearrange("p w j -> p (w j)"), N, f"k1{b}")
+
+        def empty(b, m):
+            t = keep.tile([P, N], F32, name=f"scores{b}{m}")
+            nc.scalar.copy(out=t[:], in_=acc[b, m][:])
+            return t
+
+        def place(b, m, t):
             nc.vector.tensor_tensor(
-                windows[b, m][:].indirect(offsets[:, b * COLS : (b + 1) * COLS]),
-                s[:],
-                ts_got[:, b * N : (b + 1) * N],
-                MULT,
+                windows[b, m][:].indirect(offs_of(b)), t[:], ts_got[:, b * N : (b + 1) * N], MULT
             )
             nc.sync.dma_start(out[b, m * P : (m + 1) * P, :], windows[b, m][:])
 
-        for m in range(QT):
-            mm(acc[0, m], q01, m, k10, 0, 1)
-            finish(0, m)
+        def both(b, m, q, k1):
+            mm(acc[b, m], q, 0, k0, b * N, 0)
+            mm(acc[b, m], q, P, k1, 0, 1)
 
-        q10 = quant(cast_q(1, 0), NQ, "q10")
-        for m in range(QT):
-            mm(acc[1, m], q10, m, k0, N, 0)
-        q11 = quant(cast_q(1, 1), NQ, "q11")
-        for m in range(QT):
-            mm(acc[1, m], q11, m, k11, 0, 1)
-            finish(1, m)
+        last_plane(0)
+        k10 = quant_k1(0)
+        cast_q(0, 0, 1, "scalar")
+        q01 = quant(q_flat(0, 0)[:, P * PACK :], P, "q01")
+        mm(acc[0, 0], q01, 0, k10, 0, 1)
+        last_plane(1)
+        cast_q(0, 1, 0, "scalar")
+        s00 = empty(0, 0)
+        cast_q(0, 1, 1, "vector")
+        qb = quant(q_flat(0, 1), PASSES * P, "qb")
+        both(0, 1, qb, k10)
+        place(0, 0, s00)
+        cast_q(1, 0, 0, "scalar")
+        s01 = empty(0, 1)
+        k11 = quant_k1(1)
+        cast_q(1, 0, 1, "scalar")
+        qc = quant(q_flat(1, 0), PASSES * P, "qc")
+        both(1, 0, qc, k11)
+        place(0, 1, s01)
+        cast_q(1, 1, 0, "scalar")
+        s10 = empty(1, 0)
+        cast_q(1, 1, 1, "scalar")
+        qd = quant(q_flat(1, 1), PASSES * P, "qd")
+        both(1, 1, qd, k11)
+        place(1, 0, s10)
+        s11 = empty(1, 1)
+        place(1, 1, s11)

from contextlib import ExitStack

import concourse.mybir as mybir
from concourse.masks import make_identity

B, D, NQ, T, N = 2, 1024, 256, 2048, 256
P = 128
PACK = 4
PASSES = D // (P * PACK)
QT = NQ // P
COLS = N // 16

F32 = mybir.dt.float32
BF16 = mybir.dt.bfloat16
U32 = mybir.dt.uint32
U16 = mybir.dt.uint16
U8 = mybir.dt.uint8
FP8X4 = mybir.dt.float8_e4m3fn_x4
MULT = mybir.AluOpType.mult

FLOPS = 2 * B * NQ * N * D
BYTES = 4 * (B * D * NQ + D * T + T + B * NQ * T) + 2 * P * B * COLS


def tile_attend_sddmm_srt_ts_kernel(tc, qT, kT, ts, offs, out):
    nc = tc.nc
    with ExitStack() as ctx:
        keep = ctx.enter_context(tc.tile_pool(name="keep", bufs=1))
        psum = ctx.enter_context(tc.psum_pool(name="psum", bufs=1))

        offsets = keep.tile([P, B * COLS], U16, name="offsets")
        nc.sync.dma_start(offsets[:], offs)
        ts_cols = keep.tile([P, T // P], F32, name="ts_cols")
        nc.sync.dma_start(ts_cols[:], ts[0, :].rearrange("(p i) -> p i", i=T // P))

        q_rows = qT.rearrange("b (g p j) w -> b g p j w", p=P, j=PACK)
        k_rows = kT.rearrange("(g p j) w -> g j p w", p=P, j=PACK)

        q_raw = {}
        k_raw = {}

        def load_q(b, m, g):
            t = keep.tile([P, PACK, P], F32, name=f"q_raw{b}{m}{g}")
            nc.sync.dma_start(t[:], q_rows[b, g, :, :, m * P : (m + 1) * P])
            q_raw[b, m, g] = t

        def load_k(g, j):
            t = keep.tile([P, T], F32, name=f"k_raw{g}{j}")
            nc.sync.dma_start(t[:], k_rows[g, j])
            k_raw[g, j] = t

        load_q(0, 0, 0)
        for g in range(PASSES):
            for j in range(PACK):
                load_k(g, j)
        load_q(0, 0, 1)
        for b, m in ((0, 1), (1, 0), (1, 1)):
            for g in range(PASSES):
                load_q(b, m, g)

        ident = keep.tile([P, P], F32, name="ident")
        make_identity(nc, ident[:])

        windows = {}
        for b in range(B):
            for m in range(QT):
                w = keep.tile([P, T], F32, name=f"window{b}{m}")
                (nc.vector if b == 0 else nc.gpsimd).memset(w[:], 0.0)
                windows[b, m] = w

        ts_all = keep.tile([P, T], F32, name="ts_all")
        ts_view = ts_all[:].rearrange("p (n i) -> p n i", i=T // P)
        for h in range(4):
            bank = psum.tile([P, 4, P], F32, name=f"ts_bank{h}")
            for i in range(4):
                c = 4 * h + i
                nc.tensor.transpose(bank[:, i, :], ts_cols[:, c : c + 1].to_broadcast([P, P]), ident[:])
            nc.scalar.copy(out=ts_view[:, :, 4 * h : 4 * h + 4], in_=bank[:].rearrange("p i n -> p n i"))
        ts_got = keep.tile([P, B * N], F32, name="ts_got")
        nc.vector.tensor_copy(ts_got[:], ts_all[:].indirect(offsets[:]))

        def quant(grouped, width, name):
            codes = keep.tile([P, width], U32, name=f"{name}_codes", align_bytes=64)
            scales = keep.tile([P, width], U8, name=f"{name}_scales", align_bytes=64)
            nc.vector.quantize_mx(out=codes[:].bitcast(FP8X4), scales=scales[:], in_=grouped)
            return codes, scales

        def mm(acc, q, q0, k, k0, g):
            nc.tensor.matmul_mx(
                out=acc[:],
                lhsT=q[0][:, q0 : q0 + P].bitcast(FP8X4),
                lhsT_scale=q[1][:, q0 : q0 + P],
                rhs=k[0][:, k0 : k0 + N].bitcast(FP8X4),
                rhs_scale=k[1][:, k0 : k0 + N],
                start=(g == 0),
                stop=(g == PASSES - 1),
            )

        def offs_of(b):
            return offsets[:, b * COLS : (b + 1) * COLS]

        acc, q_grouped = {}, {}
        for b in range(B):
            for m in range(QT):
                a = psum.tile([P, N], F32, name=f"acc{b}{m}")
                acc[b, m] = a
                t = keep.tile([P, PASSES, P, PACK], BF16, name=f"q_grouped{b}{m}", align_bytes=64)
                q_grouped[b, m] = t

        def cast_q(b, m, g, engine):
            src = q_raw[b, m, g][:].rearrange("p j w -> p w j")
            if engine == "scalar":
                nc.scalar.copy(out=q_grouped[b, m][:, g], in_=src)
            else:
                nc.vector.tensor_copy(q_grouped[b, m][:, g], src)

        def q_flat(b, m):
            return q_grouped[b, m][:].rearrange("p g w j -> p (g w j)")

        cast_q(0, 0, 0, "scalar")
        q00 = quant(q_flat(0, 0)[:, 0 : P * PACK], P, "q00")
        k_grouped0 = keep.tile([P, B * N, PACK], BF16, name="k_grouped0", align_bytes=64)
        for j in range(PACK):
            nc.vector.tensor_copy(k_grouped0[:, :, j], k_raw[0, j][:].indirect(offsets[:]))
        k0 = quant(k_grouped0[:].rearrange("p w j -> p (w j)"), B * N, "k0")
        mm(acc[0, 0], q00, 0, k0, 0, 0)

        k_grouped1 = []
        for b in range(B):
            t = keep.tile([P, N, PACK], BF16, name=f"k_grouped1{b}", align_bytes=64)
            k_grouped1.append(t)
        for j in range(PACK - 1):
            for b in range(B):
                nc.vector.tensor_copy(k_grouped1[b][:, :, j], k_raw[1, j][:].indirect(offs_of(b)))

        def last_plane(b):
            j = PACK - 1
            nc.vector.tensor_copy(k_grouped1[b][:, :, j], k_raw[1, j][:].indirect(offs_of(b)))

        def quant_k1(b):
            return quant(k_grouped1[b][:].rearrange("p w j -> p (w j)"), N, f"k1{b}")

        def empty(b, m):
            t = keep.tile([P, N], F32, name=f"scores{b}{m}")
            nc.scalar.copy(out=t[:], in_=acc[b, m][:])
            return t

        def place(b, m, t):
            nc.vector.tensor_tensor(
                windows[b, m][:].indirect(offs_of(b)), t[:], ts_got[:, b * N : (b + 1) * N], MULT
            )
            nc.sync.dma_start(out[b, m * P : (m + 1) * P, :], windows[b, m][:])

        def both(b, m, q, k1):
            mm(acc[b, m], q, 0, k0, b * N, 0)
            mm(acc[b, m], q, P, k1, 0, 1)

        last_plane(0)
        k10 = quant_k1(0)
        cast_q(0, 0, 1, "scalar")
        q01 = quant(q_flat(0, 0)[:, P * PACK :], P, "q01")
        mm(acc[0, 0], q01, 0, k10, 0, 1)
        last_plane(1)
        cast_q(0, 1, 0, "scalar")
        s00 = empty(0, 0)
        cast_q(0, 1, 1, "vector")
        qb = quant(q_flat(0, 1), PASSES * P, "qb")
        both(0, 1, qb, k10)
        place(0, 0, s00)
        cast_q(1, 0, 0, "scalar")
        s01 = empty(0, 1)
        k11 = quant_k1(1)
        cast_q(1, 0, 1, "scalar")
        qc = quant(q_flat(1, 0), PASSES * P, "qc")
        both(1, 0, qc, k11)
        place(0, 1, s01)
        cast_q(1, 1, 0, "scalar")
        s10 = empty(1, 0)
        cast_q(1, 1, 1, "scalar")
        qd = quant(q_flat(1, 1), PASSES * P, "qd")
        both(1, 1, qd, k11)
        place(1, 0, s10)
        s11 = empty(1, 1)
        place(1, 1, s11)
